import numpy as np
import ml_dtypes


def mxq(x, axis, fmt="e4m3"):
    dtype, down = {"e4m3": (ml_dtypes.float8_e4m3fn, 7), "e5m2": (ml_dtypes.float8_e5m2, 14)}[fmt]
    v = np.moveaxis(np.asarray(x, np.float32).astype(ml_dtypes.bfloat16).astype(np.float64), axis, -1)
    blocks = v.reshape(v.shape[:-1] + (-1, 32))
    amax = np.abs(blocks).max(-1, keepdims=True)
    byte = np.maximum(np.where(amax > 0, np.frexp(amax)[1] - 1 + 127, 0) - down, 1)
    scale = np.exp2(byte - 127.0)
    codes = (blocks / scale).astype(np.float32).astype(dtype).astype(np.float64)
    return np.moveaxis((codes * scale).reshape(v.shape), -1, axis)


WIDE = False


def mx_kscale(k):
    if not WIDE:
        return np.ones(k)
    levels = np.array([10, -10, 5, -5, 0])
    if k % 512:
        return np.exp2(np.random.permutation(np.resize(levels, k // 32))).repeat(32)
    a = np.empty((k // 512, 16))
    for p in range(k // 512):
        a[p, :8] = np.random.permutation(np.resize(levels, 8))
        for g in range(8):
            far = levels[np.abs(levels - a[p, g]) >= 10]
            a[p, g + 8] = far[np.random.randint(len(far))]
    return np.exp2(a.ravel()).repeat(32)


def f64(x):
    return np.asarray(x).astype(np.float64)


def striped(idx):
    return np.tile(idx.reshape(-1, 16).T, (8, 1)).astype(np.uint16)


def unstriped(offs):
    return offs[:16].T.reshape(-1).astype(np.int64)


def relu2(v):
    return np.maximum(v, 0.0) ** 2


K, T, E, C, H, N = 512, 4096, 12, 128, 512, 128


def by_expert(wq, xq):
    return np.concatenate([wq[e].T @ xq[:, e * C:(e + 1) * C] for e in range(E)], axis=1)


def setup_inputs():
    n = np.random.standard_normal
    s = mx_kscale(K)[:, None]
    u = mx_kscale(H)
    return {
        "xT": (n((K, T)) * s).astype(np.float32),
        "w1": (n((E, K, H)) / np.sqrt(K) / s[None] * u[None, None, :]).astype(np.float32),
        "w2": (n((E, H, N)) / np.sqrt(H) / u[None, :, None] ** 2).astype(np.float32),
        "gate": np.tile(np.random.uniform(0.2, 1.0, E * C), (N, 1)).astype(np.float32),
        "offs": striped(np.random.permutation(T)[:E * C]),
    }


def reference(xT, w1, w2, gate, offs):
    idx = unstriped(offs)
    xq = mxq(f64(xT)[:, idx], 0, "e4m3")
    h = relu2(by_expert(mxq(f64(w1), 1, "e4m3"), xq))
    y = by_expert(mxq(f64(w2), 1, "e4m3"), mxq(h, 0, "e4m3"))
    out = np.zeros((N, T))
    out[:, idx] = f64(gate) * y
    return out

@@ -1,0 +1,191 @@
+from contextlib import ExitStack
+
+import concourse.mybir as mybir
+
+K, T, E, C, H, N = 512, 4096, 12, 128, 512, 128
+FLOPS = 2 * E * C * (K * H + H * N)
+
+F32 = mybir.dt.float32
+BF16 = mybir.dt.bfloat16
+U32 = mybir.dt.uint32
+U16 = mybir.dt.uint16
+U8 = mybir.dt.uint8
+FP8X4 = mybir.dt.float8_e4m3fn_x4
+MULT = mybir.AluOpType.mult
+RELU = mybir.ActivationFunctionType.Relu
+SQUARE = mybir.ActivationFunctionType.Square
+
+P = 128
+PACK = 4
+GROUP = 4
+GROUPS = E // GROUP
+GC = GROUP * C
+SLOTS = E * C
+XCOLS = 1024
+X_CUT = 640
+W1_CUT = 64
+LEAD = 6
+
+
+def tile_routed_moe_kernel(tc, xT, w1, w2, gate, offs, out):
+    nc = tc.nc
+    with ExitStack() as ctx:
+        held = ctx.enter_context(tc.tile_pool(name="held", bufs=1))
+        xpool = ctx.enter_context(tc.tile_pool(name="xpool", bufs=4))
+        wpool = ctx.enter_context(tc.tile_pool(name="wpool", bufs=LEAD))
+        vpool = ctx.enter_context(tc.tile_pool(name="vpool", bufs=2))
+        work = ctx.enter_context(tc.tile_pool(name="work", bufs=4))
+        psum_a = ctx.enter_context(tc.psum_pool(name="psum_a", bufs=5))
+        psum_y = ctx.enter_context(tc.psum_pool(name="psum_y", bufs=2))
+
+        offsets = held.tile([P, SLOTS // 16], U16, name="offsets")
+        nc.sync.dma_start(offsets[:], offs)
+        window = held.tile([P, T], F32, name="window")
+        nc.gpsimd.memset(window[:], 0.0)
+        gates = held.tile([P, SLOTS], F32, name="gates")
+
+        pairs, grouped, xcodes = [], [], []
+        wraw, vraw, wgroup, vgroup, wcodes, vcodes = {}, {}, {}, {}, {}, {}
+        abank, ybank, relus, hidden, hcodes = {}, {}, {}, {}, {}
+
+        def group_slots(g):
+            return slice(g * GC, (g + 1) * GC)
+
+        def group_list(g):
+            return offsets[:, g * GC // 16 : (g + 1) * GC // 16]
+
+        def gather(g, u):
+            words = grouped[g][:].bitcast(U32).rearrange("p (n u) -> p n u", u=2)
+            nc.vector.tensor_copy(words[:, :, u], pairs[u][:].bitcast(U32).indirect(group_list(g)))
+
+        def quantise(pool, values, width, label):
+            codes = pool.tile([P, width], U32, name=label + "_codes", align_bytes=64)
+            scales = pool.tile([P, width], U8, name=label + "_scales", align_bytes=64)
+            nc.vector.quantize_mx(out=codes[:].bitcast(FP8X4), scales=scales[:], in_=values[:])
+            return codes, scales
+
+        def load_weights(e):
+            wraw[e] = wpool.tile([P, PACK, H], F32, name="wraw")
+            nc.sync.dma_start(wraw[e][:], w1[e].rearrange("(p j) i -> p j i", j=PACK))
+            if e % GROUP == 0:
+                g = e // GROUP
+                vraw[g] = vpool.tile([P, GROUP, PACK, N], F32, name="vraw")
+                nc.sync.dma_start(
+                    vraw[g][:], w2[g * GROUP : (g + 1) * GROUP].rearrange("e (p j) n -> p e j n", j=PACK)
+                )
+            if e == 2:
+                nc.sync.dma_start(gates[:], gate)
+
+        def interleave_w1(e):
+            wgroup[e] = work.tile([P, H * PACK], BF16, name="wgroup", align_bytes=64)
+            dst = wgroup[e][:].rearrange("p (t m j) -> p m j t", t=4, j=PACK)
+            src = wraw[e][:].rearrange("p j (m t) -> p m j t", t=4)
+            nc.scalar.copy(dst[:, W1_CUT:], src[:, W1_CUT:])
+            nc.vector.tensor_copy(dst[:, :W1_CUT], src[:, :W1_CUT])
+
+        def interleave_w2(e):
+            g, e4 = divmod(e, GROUP)
+            vgroup[e] = work.tile([P, 2 * N * PACK], BF16, name="vgroup", align_bytes=64)
+            nc.scalar.copy(
+                vgroup[e][:].rearrange("p (e c i j) -> p e c j i", e=2, i=4, j=PACK),
+                vraw[g][:, e4 : e4 + 2].rearrange("p e j (c i) -> p e c j i", i=4),
+            )
+
+        def layer1(e):
+            xq, xs = xcodes[e // GROUP]
+            wq, ws = wcodes[e]
+            slots = slice(e % GROUP * C, (e % GROUP + 1) * C)
+            abank[e] = psum_a.tile([P, 4, C], F32, name="abank")
+            for t in range(4):
+                cols = slice(t * P, (t + 1) * P)
+                nc.tensor.matmul_mx(
+                    out=abank[e][:, t, :],
+                    lhsT=wq[:, cols].bitcast(FP8X4),
+                    lhsT_scale=ws[:, cols],
+                    rhs=xq[:, slots].bitcast(FP8X4),
+                    rhs_scale=xs[:, slots],
+                    start=True,
+                    stop=True,
+                )
+
+        def relu(e):
+            relus[e] = work.tile([P, C * 4], F32, name="r")
+            nc.scalar.activation(
+                relus[e][:].rearrange("p (n t) -> p n t", t=4), abank[e][:].rearrange("p t n -> p n t"), RELU
+            )
+
+        def square(e):
+            hidden[e] = work.tile([P, C * 4], BF16, name="hidden", align_bytes=64)
+            nc.scalar.activation(hidden[e][:], relus[e][:], SQUARE)
+
+        def layer2(e):
+            g, e4 = divmod(e, GROUP)
+            if e4 == 0:
+                ybank[g] = psum_y.tile([P, GC], F32, name="ybank")
+            vq, vs = vcodes[e - e % 2]
+            hq, hs = hcodes[e]
+            cols = slice(e % 2 * N, (e % 2 + 1) * N)
+            nc.tensor.matmul_mx(
+                out=ybank[g][:, e4 * C : (e4 + 1) * C],
+                lhsT=vq[:, cols].bitcast(FP8X4),
+                lhsT_scale=vs[:, cols],
+                rhs=hq[:].bitcast(FP8X4),
+                rhs_scale=hs[:],
+                start=True,
+                stop=True,
+            )
+
+        def way_back(g):
+            y = vpool.tile([P, GC], F32, name="y")
+            nc.scalar.copy(y[:], ybank[g][:])
+            nc.vector.tensor_tensor(window[:].indirect(group_list(g)), y[:], gates[:, group_slots(g)], MULT)
+
+        rows = xT.rearrange("(p j) n -> p j n", j=PACK)
+        for g in range(GROUPS):
+            xg = work.tile([P, GC * PACK], BF16, name="xg", align_bytes=64)
+            grouped.append(xg)
+        for u in range(2):
+            pair = held.tile([P, 2 * T], BF16, name=f"pair{u}", align_bytes=64)
+            pairs.append(pair)
+            for c in range(T // XCOLS):
+                cols = slice(c * XCOLS, (c + 1) * XCOLS)
+                xraw = xpool.tile([P, 2, XCOLS], F32, name="xraw")
+                nc.sync.dma_start(xraw[:], rows[:, 2 * u : 2 * u + 2, cols])
+                dst = pair[:].rearrange("p (t e) -> p t e", e=2)[:, cols, :]
+                src = xraw[:].rearrange("p e t -> p t e")
+                nc.scalar.copy(dst[:, :X_CUT, :], src[:, :X_CUT, :])
+                nc.vector.tensor_copy(dst[:, X_CUT:, :], src[:, X_CUT:, :])
+            if u == 0:
+                for g in range(GROUPS):
+                    gather(g, 0)
+        for e in range(LEAD):
+            load_weights(e)
+
+        for s in range(-3, E + 3):
+            if s == -3:
+                gather(0, 1)
+            if s in (-1, 3):
+                gather((s + 1) // 4 + 1, 1)
+            if 0 <= s < E:
+                relu(s)
+            if 0 <= s - 2 < E:
+                hcodes[s - 2] = quantise(work, hidden[s - 2], C, "h")
+                layer2(s - 2)
+            if s % GROUP == 2 and s > 2:
+                way_back(s // GROUP - 1)
+            if s + 3 < E:
+                interleave_w1(s + 3)
+                if (s + 3) % 2 == 0:
+                    interleave_w2(s + 3)
+                if s + 3 + LEAD < E:
+                    load_weights(s + 3 + LEAD)
+            if s in (-3, 1, 5):
+                xcodes.append(quantise(work, grouped[(s + 3) // 4], GC, "x"))
+            if 0 <= s + 2 < E:
+                wcodes[s + 2] = quantise(work, wgroup[s + 2], H, "w1")
+                layer1(s + 2)
+                if (s + 2) % 2 == 0:
+                    vcodes[s + 2] = quantise(work, vgroup[s + 2], 2 * N, "w2")
+            if 0 <= s < E:
+                square(s)
+        nc.sync.dma_start(out, window[:])

@@ -21,22 +21,23 @@ GROUP = 4
 GROUPS = E // GROUP
 GC = GROUP * C
 SLOTS = E * C
-XCOLS = 1024
-X_CUT = 640
-W1_CUT = 64
-LEAD = 6
+X_RAW, W1_RAW, W2_RAW, W1_VALS, W2_VALS = 4, 5, 3, 4, 1
+W1_CODES, W2_CODES, A_BANKS, RELUS, HIDDEN, H_CODES = 2, 2, 6, 3, 3, 4
+W2_RUN = 4
+X_CHUNKS = [[(1024, 512), (1024, 512), (1024, 512), (1024, 512)], [(1024, 512), (1024, 512), (1024, 512), (1024, 512)]]
+W1_CUT = [80, 64, 128, 96, 32, 48, 128, 128, 0, 16, 128, 128]
+W2_CUT = {0: 4, 4: 4, 8: 1}
+RELU_CUT = [64, 64, 128, 64, 128, 128, 128, 128, 128, 128, 128, 128]
+SQUARE_CUT = [0, 0, 0, 0, 0, 64, 128, 128, 64, 0, 64, 64]
+Y_PIECES = [[('S', 0, 3), ('S', 3, 4)], [('S', 0, 3), ('S', 3, 4)], [('S', 0, 3), ('S', 3, 4)]]
 
 
 def tile_routed_moe_kernel(tc, xT, w1, w2, gate, offs, out):
     nc = tc.nc
     with ExitStack() as ctx:
         held = ctx.enter_context(tc.tile_pool(name="held", bufs=1))
-        xpool = ctx.enter_context(tc.tile_pool(name="xpool", bufs=4))
-        wpool = ctx.enter_context(tc.tile_pool(name="wpool", bufs=LEAD))
-        vpool = ctx.enter_context(tc.tile_pool(name="vpool", bufs=2))
-        work = ctx.enter_context(tc.tile_pool(name="work", bufs=4))
-        psum_a = ctx.enter_context(tc.psum_pool(name="psum_a", bufs=5))
-        psum_y = ctx.enter_context(tc.psum_pool(name="psum_y", bufs=2))
+        ring = ctx.enter_context(tc.tile_pool(name="ring", bufs=2))
+        psum = ctx.enter_context(tc.psum_pool(name="psum", bufs=2))
 
         offsets = held.tile([P, SLOTS // 16], U16, name="offsets")
         nc.sync.dma_start(offsets[:], offs)
@@ -44,9 +45,9 @@ def tile_routed_moe_kernel(tc, xT, w1, w2, gate, offs, out):
         nc.gpsimd.memset(window[:], 0.0)
         gates = held.tile([P, SLOTS], F32, name="gates")
 
-        pairs, grouped, xcodes = [], [], []
-        wraw, vraw, wgroup, vgroup, wcodes, vcodes = {}, {}, {}, {}, {}, {}
-        abank, ybank, relus, hidden, hcodes = {}, {}, {}, {}, {}
+        pairs, grouped = [], []
+        xcodes, w1raw, w2raw, w1vals, w2vals, w1codes, w2codes = {}, {}, {}, {}, {}, {}, {}
+        abank, ybank, relus, hidden = {}, {}, {}, {}
 
         def group_slots(g):
             return slice(g * GC, (g + 1) * GC)
@@ -58,44 +59,51 @@ def tile_routed_moe_kernel(tc, xT, w1, w2, gate, offs, out):
             words = grouped[g][:].bitcast(U32).rearrange("p (n u) -> p n u", u=2)
             nc.vector.tensor_copy(words[:, :, u], pairs[u][:].bitcast(U32).indirect(group_list(g)))
 
-        def quantise(pool, values, width, label):
-            codes = pool.tile([P, width], U32, name=label + "_codes", align_bytes=64)
-            scales = pool.tile([P, width], U8, name=label + "_scales", align_bytes=64)
+        def quantise(values, width, label, bufs):
+            codes = ring.tile([P, width], U32, name=label + "_codes", align_bytes=64, bufs=bufs)
+            scales = ring.tile([P, width], U8, name=label + "_scales", align_bytes=64, bufs=bufs)
             nc.vector.quantize_mx(out=codes[:].bitcast(FP8X4), scales=scales[:], in_=values[:])
             return codes, scales
 
-        def load_weights(e):
-            wraw[e] = wpool.tile([P, PACK, H], F32, name="wraw")
-            nc.sync.dma_start(wraw[e][:], w1[e].rearrange("(p j) i -> p j i", j=PACK))
-            if e % GROUP == 0:
-                g = e // GROUP
-                vraw[g] = vpool.tile([P, GROUP, PACK, N], F32, name="vraw")
-                nc.sync.dma_start(
-                    vraw[g][:], w2[g * GROUP : (g + 1) * GROUP].rearrange("e (p j) n -> p e j n", j=PACK)
-                )
-            if e == 2:
-                nc.sync.dma_start(gates[:], gate)
+        def split_copy(dst, src, cut):
+            if cut > 0:
+                nc.scalar.copy(dst[:, :cut], src[:, :cut])
+            if cut < dst.shape[1]:
+                nc.vector.tensor_copy(dst[:, cut:], src[:, cut:])
+
+        def load_w1(e):
+            w1raw[e] = ring.tile([P, PACK, H], F32, name="w1raw", bufs=W1_RAW)
+            nc.sync.dma_start(w1raw[e][:], w1[e].rearrange("(p j) i -> p j i", j=PACK))
+
+        def load_w2(k):
+            w2raw[k] = ring.tile([P, W2_RUN, PACK, N], F32, name="w2raw", bufs=W2_RAW)
+            nc.sync.dma_start(w2raw[k][:], w2[k : k + W2_RUN].rearrange("e (p j) n -> p e j n", j=PACK))
+
+        def load_gates(g):
+            nc.sync.dma_start(gates[:, group_slots(g)], gate[:, group_slots(g)])
 
         def interleave_w1(e):
-            wgroup[e] = work.tile([P, H * PACK], BF16, name="wgroup", align_bytes=64)
-            dst = wgroup[e][:].rearrange("p (t m j) -> p m j t", t=4, j=PACK)
-            src = wraw[e][:].rearrange("p j (m t) -> p m j t", t=4)
-            nc.scalar.copy(dst[:, W1_CUT:], src[:, W1_CUT:])
-            nc.vector.tensor_copy(dst[:, :W1_CUT], src[:, :W1_CUT])
+            w1vals[e] = ring.tile([P, H * PACK], BF16, name="w1vals", align_bytes=64, bufs=W1_VALS)
+            split_copy(
+                w1vals[e][:].rearrange("p (t m j) -> p m j t", t=4, j=PACK),
+                w1raw[e][:].rearrange("p j (m t) -> p m j t", t=4),
+                W1_CUT[e],
+            )
 
-        def interleave_w2(e):
-            g, e4 = divmod(e, GROUP)
-            vgroup[e] = work.tile([P, 2 * N * PACK], BF16, name="vgroup", align_bytes=64)
-            nc.scalar.copy(
-                vgroup[e][:].rearrange("p (e c i j) -> p e c j i", e=2, i=4, j=PACK),
-                vraw[g][:, e4 : e4 + 2].rearrange("p e j (c i) -> p e c j i", i=4),
+        def interleave_w2(k):
+            w2vals[k] = ring.tile([P, W2_RUN * N * PACK], BF16, name="w2vals", align_bytes=64, bufs=W2_VALS)
+            split_copy(
+                w2vals[k][:].rearrange("p (e c i j) -> p e c j i", e=W2_RUN, i=4, j=PACK),
+                w2raw[k][:].rearrange("p e j (c i) -> p e c j i", i=4),
+                W2_CUT[k],
             )
 
         def layer1(e):
+            w1codes[e] = quantise(w1vals[e], H, "w1", W1_CODES)
+            wq, ws = w1codes[e]
             xq, xs = xcodes[e // GROUP]
-            wq, ws = wcodes[e]
             slots = slice(e % GROUP * C, (e % GROUP + 1) * C)
-            abank[e] = psum_a.tile([P, 4, C], F32, name="abank")
+            abank[e] = psum.tile([P, 4, C], F32, name="abank", bufs=A_BANKS)
             for t in range(4):
                 cols = slice(t * P, (t + 1) * P)
                 nc.tensor.matmul_mx(
@@ -109,22 +117,30 @@ def tile_routed_moe_kernel(tc, xT, w1, w2, gate, offs, out):
                 )
 
         def relu(e):
-            relus[e] = work.tile([P, C * 4], F32, name="r")
-            nc.scalar.activation(
-                relus[e][:].rearrange("p (n t) -> p n t", t=4), abank[e][:].rearrange("p t n -> p n t"), RELU
-            )
+            relus[e] = ring.tile([P, C * 4], F32, name="relus", bufs=RELUS)
+            dst = relus[e][:].rearrange("p (n t) -> p n t", t=4)
+            src = abank[e][:].rearrange("p t n -> p n t")
+            cut = RELU_CUT[e]
+            if cut > 0:
+                nc.scalar.activation(dst[:, :cut], src[:, :cut], RELU)
+            if cut < C:
+                nc.vector.tensor_scalar_max(dst[:, cut:], src[:, cut:], 0.0)
 
         def square(e):
-            hidden[e] = work.tile([P, C * 4], BF16, name="hidden", align_bytes=64)
-            nc.scalar.activation(hidden[e][:], relus[e][:], SQUARE)
+            hidden[e] = ring.tile([P, C * 4], BF16, name="hidden", align_bytes=64, bufs=HIDDEN)
+            cut = SQUARE_CUT[e] * 4
+            if cut > 0:
+                nc.scalar.activation(hidden[e][:, :cut], relus[e][:, :cut], SQUARE)
+            if cut < C * 4:
+                nc.vector.tensor_tensor(hidden[e][:, cut:], relus[e][:, cut:], relus[e][:, cut:], MULT)
 
         def layer2(e):
             g, e4 = divmod(e, GROUP)
             if e4 == 0:
-                ybank[g] = psum_y.tile([P, GC], F32, name="ybank")
-            vq, vs = vcodes[e - e % 2]
-            hq, hs = hcodes[e]
-            cols = slice(e % 2 * N, (e % 2 + 1) * N)
+                ybank[g] = psum.tile([P, GC], F32, name="ybank", bufs=2)
+            hq, hs = quantise(hidden[e], C, "hidden", H_CODES)
+            vq, vs = w2codes[e - e % W2_RUN]
+            cols = slice(e % W2_RUN * N, (e % W2_RUN + 1) * N)
             nc.tensor.matmul_mx(
                 out=ybank[g][:, e4 * C : (e4 + 1) * C],
                 lhsT=vq[:, cols].bitcast(FP8X4),
@@ -136,56 +152,127 @@ def tile_routed_moe_kernel(tc, xT, w1, w2, gate, offs, out):
             )
 
         def way_back(g):
-            y = vpool.tile([P, GC], F32, name="y")
-            nc.scalar.copy(y[:], ybank[g][:])
+            y = ring.tile([P, GC], F32, name="y", bufs=2)
+            for engine, a, b in Y_PIECES[g]:
+                if engine == "S":
+                    nc.scalar.copy(y[:, a * C : b * C], ybank[g][:, a * C : b * C])
+                else:
+                    nc.vector.tensor_copy(y[:, a * C : b * C], ybank[g][:, a * C : b * C])
             nc.vector.tensor_tensor(window[:].indirect(group_list(g)), y[:], gates[:, group_slots(g)], MULT)
 
         rows = xT.rearrange("(p j) n -> p j n", j=PACK)
         for g in range(GROUPS):
-            xg = work.tile([P, GC * PACK], BF16, name="xg", align_bytes=64)
+            xg = ring.tile([P, GC * PACK], BF16, name="xg", align_bytes=64, bufs=GROUPS)
             grouped.append(xg)
         for u in range(2):
             pair = held.tile([P, 2 * T], BF16, name=f"pair{u}", align_bytes=64)
             pairs.append(pair)
-            for c in range(T // XCOLS):
-                cols = slice(c * XCOLS, (c + 1) * XCOLS)
-                xraw = xpool.tile([P, 2, XCOLS], F32, name="xraw")
+            first = 0
+            for width, cut in X_CHUNKS[u]:
+                cols = slice(first, first + width)
+                first += width
+                xraw = ring.tile([P, 2, width], F32, name="xraw", bufs=X_RAW)
                 nc.sync.dma_start(xraw[:], rows[:, 2 * u : 2 * u + 2, cols])
-                dst = pair[:].rearrange("p (t e) -> p t e", e=2)[:, cols, :]
-                src = xraw[:].rearrange("p e t -> p t e")
-                nc.scalar.copy(dst[:, :X_CUT, :], src[:, :X_CUT, :])
-                nc.vector.tensor_copy(dst[:, X_CUT:, :], src[:, X_CUT:, :])
+                split_copy(
+                    pair[:].rearrange("p (t e) -> p t e", e=2)[:, cols, :],
+                    xraw[:].rearrange("p e t -> p t e"),
+                    cut,
+                )
             if u == 0:
                 for g in range(GROUPS):
                     gather(g, 0)
-        for e in range(LEAD):
-            load_weights(e)
 
-        for s in range(-3, E + 3):
-            if s == -3:
-                gather(0, 1)
-            if s in (-1, 3):
-                gather((s + 1) // 4 + 1, 1)
-            if 0 <= s < E:
-                relu(s)
-            if 0 <= s - 2 < E:
-                hcodes[s - 2] = quantise(work, hidden[s - 2], C, "h")
-                layer2(s - 2)
-            if s % GROUP == 2 and s > 2:
-                way_back(s // GROUP - 1)
-            if s + 3 < E:
-                interleave_w1(s + 3)
-                if (s + 3) % 2 == 0:
-                    interleave_w2(s + 3)
-                if s + 3 + LEAD < E:
-                    load_weights(s + 3 + LEAD)
-            if s in (-3, 1, 5):
-                xcodes.append(quantise(work, grouped[(s + 3) // 4], GC, "x"))
-            if 0 <= s + 2 < E:
-                wcodes[s + 2] = quantise(work, wgroup[s + 2], H, "w1")
-                layer1(s + 2)
-                if (s + 2) % 2 == 0:
-                    vcodes[s + 2] = quantise(work, vgroup[s + 2], 2 * N, "w2")
-            if 0 <= s < E:
-                square(s)
+        load_w1(0)
+        load_w2(0)
+        load_w1(1)
+        load_w1(2)
+        load_gates(0)
+        load_w1(3)
+        load_w1(4)
+        gather(0, 1)
+        xcodes[0] = quantise(grouped[0], GC, "x", GROUPS)
+        gather(1, 1)
+        interleave_w1(0)
+        load_w2(4)
+        load_w1(5)
+        xcodes[1] = quantise(grouped[1], GC, "x", GROUPS)
+        interleave_w2(0)
+        layer1(0)
+        interleave_w1(1)
+        load_w1(6)
+        relu(0)
+        layer1(1)
+        interleave_w1(2)
+        load_gates(1)
+        load_w1(7)
+        relu(1)
+        square(0)
+        w2codes[0] = quantise(w2vals[0], W2_RUN * N, "w2", W2_CODES)
+        layer1(2)
+        layer2(0)
+        interleave_w1(3)
+        load_w1(8)
+        relu(2)
+        square(1)
+        gather(2, 1)
+        layer1(3)
+        layer2(1)
+        interleave_w1(4)
+        load_w1(9)
+        relu(3)
+        square(2)
+        xcodes[2] = quantise(grouped[2], GC, "x", GROUPS)
+        interleave_w2(4)
+        layer1(4)
+        layer2(2)
+        interleave_w1(5)
+        load_w1(10)
+        relu(4)
+        square(3)
+        layer1(5)
+        layer2(3)
+        interleave_w1(6)
+        load_w1(11)
+        load_w2(8)
+        load_gates(2)
+        relu(5)
+        square(4)
+        w2codes[4] = quantise(w2vals[4], W2_RUN * N, "w2", W2_CODES)
+        way_back(0)
+        layer1(6)
+        layer2(4)
+        interleave_w1(7)
+        relu(6)
+        square(5)
+        layer1(7)
+        layer2(5)
+        interleave_w1(8)
+        relu(7)
+        square(6)
+        interleave_w2(8)
+        layer1(8)
+        layer2(6)
+        interleave_w1(9)
+        relu(8)
+        square(7)
+        layer1(9)
+        layer2(7)
+        interleave_w1(10)
+        relu(9)
+        square(8)
+        w2codes[8] = quantise(w2vals[8], W2_RUN * N, "w2", W2_CODES)
+        way_back(1)
+        layer1(10)
+        layer2(8)
+        interleave_w1(11)
+        relu(10)
+        square(9)
+        layer1(11)
+        layer2(9)
+        relu(11)
+        square(10)
+        layer2(10)
+        square(11)
+        layer2(11)
+        way_back(2)
         nc.sync.dma_start(out, window[:])

@@ -21,15 +21,16 @@ GROUP = 4
 GROUPS = E // GROUP
 GC = GROUP * C
 SLOTS = E * C
-X_RAW, W1_RAW, W2_RAW, W1_VALS, W2_VALS = 4, 5, 3, 4, 1
-W1_CODES, W2_CODES, A_BANKS, RELUS, HIDDEN, H_CODES = 2, 2, 6, 3, 3, 4
+X_RAW, W1_RAW, W2_RAW, W1_VALS, W2_VALS = 3, 4, 2, 2, 1
+W1_CODES, W2_CODES, A_BANKS, RELUS, HIDDEN, H_CODES = 3, 2, 6, 4, 3, 4
+X_GROUPS = [(0, 4), (4, 12)]
 W2_RUN = 4
-X_CHUNKS = [[(1024, 512), (1024, 512), (1024, 512), (1024, 512)], [(1024, 512), (1024, 512), (1024, 512), (1024, 512)]]
-W1_CUT = [80, 64, 128, 96, 32, 48, 128, 128, 0, 16, 128, 128]
+X_CHUNKS = [[(2048, 1024), (2048, 1024)], [(2048, 1024), (1024, 512), (1024, 512)]]
+W1_CUT = [128, 112, 128, 96, 64, 32, 128, 128, 32, 64, 128, 32]
 W2_CUT = {0: 4, 4: 4, 8: 1}
-RELU_CUT = [64, 64, 128, 64, 128, 128, 128, 128, 128, 128, 128, 128]
-SQUARE_CUT = [0, 0, 0, 0, 0, 64, 128, 128, 64, 0, 64, 64]
-Y_PIECES = [[('S', 0, 3), ('S', 3, 4)], [('S', 0, 3), ('S', 3, 4)], [('S', 0, 3), ('S', 3, 4)]]
+RELU_CUT = [0, 64, 128, 0, 128, 128, 128, 128, 128, 128, 128, 128]
+SQUARE_CUT = [0, 0, 0, 0, 0, 0, 0, 128, 128, 128, 128, 64]
+Y_PIECES = [[('S', 0, 3), ('S', 3, 4)], [('V', 0, 4)], [('S', 0, 3), ('S', 3, 4)]]
 
 
 def tile_routed_moe_kernel(tc, xT, w1, w2, gate, offs, out):
@@ -52,12 +53,11 @@ def tile_routed_moe_kernel(tc, xT, w1, w2, gate, offs, out):
         def group_slots(g):
             return slice(g * GC, (g + 1) * GC)
 
-        def group_list(g):
-            return offsets[:, g * GC // 16 : (g + 1) * GC // 16]
-
         def gather(g, u):
+            first, last = X_GROUPS[g]
             words = grouped[g][:].bitcast(U32).rearrange("p (n u) -> p n u", u=2)
-            nc.vector.tensor_copy(words[:, :, u], pairs[u][:].bitcast(U32).indirect(group_list(g)))
+            lists = offsets[:, first * C // 16 : last * C // 16]
+            nc.vector.tensor_copy(words[:, :, u], pairs[u][:].bitcast(U32).indirect(lists))
 
         def quantise(values, width, label, bufs):
             codes = ring.tile([P, width], U32, name=label + "_codes", align_bytes=64, bufs=bufs)
@@ -101,8 +101,8 @@ def tile_routed_moe_kernel(tc, xT, w1, w2, gate, offs, out):
         def layer1(e):
             w1codes[e] = quantise(w1vals[e], H, "w1", W1_CODES)
             wq, ws = w1codes[e]
-            xq, xs = xcodes[e // GROUP]
-            slots = slice(e % GROUP * C, (e % GROUP + 1) * C)
+            first, xq, xs = [(X_GROUPS[g][0], *xcodes[g]) for g in xcodes if X_GROUPS[g][0] <= e < X_GROUPS[g][1]][0]
+            slots = slice((e - first) * C, (e - first + 1) * C)
             abank[e] = psum.tile([P, 4, C], F32, name="abank", bufs=A_BANKS)
             for t in range(4):
                 cols = slice(t * P, (t + 1) * P)
@@ -158,11 +158,11 @@ def tile_routed_moe_kernel(tc, xT, w1, w2, gate, offs, out):
                     nc.scalar.copy(y[:, a * C : b * C], ybank[g][:, a * C : b * C])
                 else:
                     nc.vector.tensor_copy(y[:, a * C : b * C], ybank[g][:, a * C : b * C])
-            nc.vector.tensor_tensor(window[:].indirect(group_list(g)), y[:], gates[:, group_slots(g)], MULT)
+            nc.vector.tensor_tensor(window[:].indirect(offsets[:, g * GC // 16 : (g + 1) * GC // 16]), y[:], gates[:, group_slots(g)], MULT)
 
         rows = xT.rearrange("(p j) n -> p j n", j=PACK)
-        for g in range(GROUPS):
-            xg = ring.tile([P, GC * PACK], BF16, name="xg", align_bytes=64, bufs=GROUPS)
+        for g, (first, last) in enumerate(X_GROUPS):
+            xg = held.tile([P, (last - first) * C * PACK], BF16, name=f"xg{g}", align_bytes=64)
             grouped.append(xg)
         for u in range(2):
             pair = held.tile([P, 2 * T], BF16, name=f"pair{u}", align_bytes=64)
@@ -179,7 +179,7 @@ def tile_routed_moe_kernel(tc, xT, w1, w2, gate, offs, out):
                     cut,
                 )
             if u == 0:
-                for g in range(GROUPS):
+                for g in range(len(X_GROUPS)):
                     gather(g, 0)
 
         load_w1(0)
@@ -188,91 +188,89 @@ def tile_routed_moe_kernel(tc, xT, w1, w2, gate, offs, out):
         load_w1(2)
         load_gates(0)
         load_w1(3)
-        load_w1(4)
         gather(0, 1)
-        xcodes[0] = quantise(grouped[0], GC, "x", GROUPS)
-        gather(1, 1)
+        xcodes[0] = quantise(grouped[0], 512, "x0", 1)
         interleave_w1(0)
-        load_w2(4)
-        load_w1(5)
-        xcodes[1] = quantise(grouped[1], GC, "x", GROUPS)
-        interleave_w2(0)
+        load_w1(4)
         layer1(0)
         interleave_w1(1)
-        load_w1(6)
-        relu(0)
+        load_w2(4)
+        load_w1(5)
         layer1(1)
         interleave_w1(2)
+        load_w1(6)
+        gather(1, 1)
+        layer1(2)
+        xcodes[1] = quantise(grouped[1], 1024, "x1", 1)
+        interleave_w1(3)
         load_gates(1)
         load_w1(7)
-        relu(1)
-        square(0)
-        w2codes[0] = quantise(w2vals[0], W2_RUN * N, "w2", W2_CODES)
-        layer1(2)
-        layer2(0)
-        interleave_w1(3)
-        load_w1(8)
-        relu(2)
-        square(1)
-        gather(2, 1)
+        relu(0)
         layer1(3)
-        layer2(1)
         interleave_w1(4)
-        load_w1(9)
-        relu(3)
-        square(2)
-        xcodes[2] = quantise(grouped[2], GC, "x", GROUPS)
-        interleave_w2(4)
+        load_w1(8)
+        square(0)
+        relu(1)
+        interleave_w2(0)
         layer1(4)
-        layer2(2)
         interleave_w1(5)
-        load_w1(10)
-        relu(4)
-        square(3)
+        load_w1(9)
+        w2codes[0] = quantise(w2vals[0], W2_RUN * N, "w2", W2_CODES)
+        square(1)
+        relu(2)
         layer1(5)
-        layer2(3)
+        layer2(0)
         interleave_w1(6)
+        load_w1(10)
+        square(2)
+        relu(3)
+        layer1(6)
+        layer2(1)
+        interleave_w1(7)
         load_w1(11)
         load_w2(8)
         load_gates(2)
-        relu(5)
-        square(4)
-        w2codes[4] = quantise(w2vals[4], W2_RUN * N, "w2", W2_CODES)
-        way_back(0)
-        layer1(6)
-        layer2(4)
-        interleave_w1(7)
-        relu(6)
-        square(5)
+        square(3)
+        relu(4)
         layer1(7)
-        layer2(5)
+        layer2(2)
         interleave_w1(8)
-        relu(7)
-        square(6)
-        interleave_w2(8)
+        square(4)
+        relu(5)
+        interleave_w2(4)
         layer1(8)
-        layer2(6)
+        layer2(3)
+        way_back(0)
         interleave_w1(9)
-        relu(8)
-        square(7)
+        w2codes[4] = quantise(w2vals[4], W2_RUN * N, "w2", W2_CODES)
+        square(5)
+        relu(6)
         layer1(9)
-        layer2(7)
+        layer2(4)
         interleave_w1(10)
-        relu(9)
-        square(8)
-        w2codes[8] = quantise(w2vals[8], W2_RUN * N, "w2", W2_CODES)
-        way_back(1)
+        square(6)
+        relu(7)
         layer1(10)
-        layer2(8)
+        layer2(5)
         interleave_w1(11)
-        relu(10)
-        square(9)
+        square(7)
+        relu(8)
         layer1(11)
-        layer2(9)
-        relu(11)
+        layer2(6)
+        square(8)
+        relu(9)
+        interleave_w2(8)
+        layer2(7)
+        way_back(1)
+        w2codes[8] = quantise(w2vals[8], W2_RUN * N, "w2", W2_CODES)
+        square(9)
+        relu(10)
+        layer2(8)
         square(10)
-        layer2(10)
+        relu(11)
+        layer2(9)
         square(11)
+        layer2(10)
         layer2(11)
         way_back(2)
         nc.sync.dma_start(out, window[:])

from contextlib import ExitStack

import concourse.mybir as mybir

K, T, E, C, H, N = 512, 4096, 12, 128, 512, 128
FLOPS = 2 * E * C * (K * H + H * N)

F32 = mybir.dt.float32
BF16 = mybir.dt.bfloat16
U32 = mybir.dt.uint32
U16 = mybir.dt.uint16
U8 = mybir.dt.uint8
FP8X4 = mybir.dt.float8_e4m3fn_x4
MULT = mybir.AluOpType.mult
RELU = mybir.ActivationFunctionType.Relu
SQUARE = mybir.ActivationFunctionType.Square

P = 128
PACK = 4
GROUP = 4
GROUPS = E // GROUP
GC = GROUP * C
SLOTS = E * C
X_RAW, W1_RAW, W2_RAW, W1_VALS, W2_VALS = 3, 4, 2, 2, 1
W1_CODES, W2_CODES, A_BANKS, RELUS, HIDDEN, H_CODES = 3, 2, 6, 4, 3, 4
X_GROUPS = [(0, 4), (4, 12)]
W2_RUN = 4
X_CHUNKS = [[(2048, 1024), (2048, 1024)], [(2048, 1024), (1024, 512), (1024, 512)]]
W1_CUT = [128, 112, 128, 96, 64, 32, 128, 128, 32, 64, 128, 32]
W2_CUT = {0: 4, 4: 4, 8: 1}
RELU_CUT = [0, 64, 128, 0, 128, 128, 128, 128, 128, 128, 128, 128]
SQUARE_CUT = [0, 0, 0, 0, 0, 0, 0, 128, 128, 128, 128, 64]
Y_PIECES = [[('S', 0, 3), ('S', 3, 4)], [('V', 0, 4)], [('S', 0, 3), ('S', 3, 4)]]


def tile_routed_moe_kernel(tc, xT, w1, w2, gate, offs, out):
    nc = tc.nc
    with ExitStack() as ctx:
        held = ctx.enter_context(tc.tile_pool(name="held", bufs=1))
        ring = ctx.enter_context(tc.tile_pool(name="ring", bufs=2))
        psum = ctx.enter_context(tc.psum_pool(name="psum", bufs=2))

        offsets = held.tile([P, SLOTS // 16], U16, name="offsets")
        nc.sync.dma_start(offsets[:], offs)
        window = held.tile([P, T], F32, name="window")
        nc.gpsimd.memset(window[:], 0.0)
        gates = held.tile([P, SLOTS], F32, name="gates")

        pairs, grouped = [], []
        xcodes, w1raw, w2raw, w1vals, w2vals, w1codes, w2codes = {}, {}, {}, {}, {}, {}, {}
        abank, ybank, relus, hidden = {}, {}, {}, {}

        def group_slots(g):
            return slice(g * GC, (g + 1) * GC)

        def gather(g, u):
            first, last = X_GROUPS[g]
            words = grouped[g][:].bitcast(U32).rearrange("p (n u) -> p n u", u=2)
            lists = offsets[:, first * C // 16 : last * C // 16]
            nc.vector.tensor_copy(words[:, :, u], pairs[u][:].bitcast(U32).indirect(lists))

        def quantise(values, width, label, bufs):
            codes = ring.tile([P, width], U32, name=label + "_codes", align_bytes=64, bufs=bufs)
            scales = ring.tile([P, width], U8, name=label + "_scales", align_bytes=64, bufs=bufs)
            nc.vector.quantize_mx(out=codes[:].bitcast(FP8X4), scales=scales[:], in_=values[:])
            return codes, scales

        def split_copy(dst, src, cut):
            if cut > 0:
                nc.scalar.copy(dst[:, :cut], src[:, :cut])
            if cut < dst.shape[1]:
                nc.vector.tensor_copy(dst[:, cut:], src[:, cut:])

        def load_w1(e):
            w1raw[e] = ring.tile([P, PACK, H], F32, name="w1raw", bufs=W1_RAW)
            nc.sync.dma_start(w1raw[e][:], w1[e].rearrange("(p j) i -> p j i", j=PACK))

        def load_w2(k):
            w2raw[k] = ring.tile([P, W2_RUN, PACK, N], F32, name="w2raw", bufs=W2_RAW)
            nc.sync.dma_start(w2raw[k][:], w2[k : k + W2_RUN].rearrange("e (p j) n -> p e j n", j=PACK))

        def load_gates(g):
            nc.sync.dma_start(gates[:, group_slots(g)], gate[:, group_slots(g)])

        def interleave_w1(e):
            w1vals[e] = ring.tile([P, H * PACK], BF16, name="w1vals", align_bytes=64, bufs=W1_VALS)
            split_copy(
                w1vals[e][:].rearrange("p (t m j) -> p m j t", t=4, j=PACK),
                w1raw[e][:].rearrange("p j (m t) -> p m j t", t=4),
                W1_CUT[e],
            )

        def interleave_w2(k):
            w2vals[k] = ring.tile([P, W2_RUN * N * PACK], BF16, name="w2vals", align_bytes=64, bufs=W2_VALS)
            split_copy(
                w2vals[k][:].rearrange("p (e c i j) -> p e c j i", e=W2_RUN, i=4, j=PACK),
                w2raw[k][:].rearrange("p e j (c i) -> p e c j i", i=4),
                W2_CUT[k],
            )

        def layer1(e):
            w1codes[e] = quantise(w1vals[e], H, "w1", W1_CODES)
            wq, ws = w1codes[e]
            first, xq, xs = [(X_GROUPS[g][0], *xcodes[g]) for g in xcodes if X_GROUPS[g][0] <= e < X_GROUPS[g][1]][0]
            slots = slice((e - first) * C, (e - first + 1) * C)
            abank[e] = psum.tile([P, 4, C], F32, name="abank", bufs=A_BANKS)
            for t in range(4):
                cols = slice(t * P, (t + 1) * P)
                nc.tensor.matmul_mx(
                    out=abank[e][:, t, :],
                    lhsT=wq[:, cols].bitcast(FP8X4),
                    lhsT_scale=ws[:, cols],
                    rhs=xq[:, slots].bitcast(FP8X4),
                    rhs_scale=xs[:, slots],
                    start=True,
                    stop=True,
                )

        def relu(e):
            relus[e] = ring.tile([P, C * 4], F32, name="relus", bufs=RELUS)
            dst = relus[e][:].rearrange("p (n t) -> p n t", t=4)
            src = abank[e][:].rearrange("p t n -> p n t")
            cut = RELU_CUT[e]
            if cut > 0:
                nc.scalar.activation(dst[:, :cut], src[:, :cut], RELU)
            if cut < C:
                nc.vector.tensor_scalar_max(dst[:, cut:], src[:, cut:], 0.0)

        def square(e):
            hidden[e] = ring.tile([P, C * 4], BF16, name="hidden", align_bytes=64, bufs=HIDDEN)
            cut = SQUARE_CUT[e] * 4
            if cut > 0:
                nc.scalar.activation(hidden[e][:, :cut], relus[e][:, :cut], SQUARE)
            if cut < C * 4:
                nc.vector.tensor_tensor(hidden[e][:, cut:], relus[e][:, cut:], relus[e][:, cut:], MULT)

        def layer2(e):
            g, e4 = divmod(e, GROUP)
            if e4 == 0:
                ybank[g] = psum.tile([P, GC], F32, name="ybank", bufs=2)
            hq, hs = quantise(hidden[e], C, "hidden", H_CODES)
            vq, vs = w2codes[e - e % W2_RUN]
            cols = slice(e % W2_RUN * N, (e % W2_RUN + 1) * N)
            nc.tensor.matmul_mx(
                out=ybank[g][:, e4 * C : (e4 + 1) * C],
                lhsT=vq[:, cols].bitcast(FP8X4),
                lhsT_scale=vs[:, cols],
                rhs=hq[:].bitcast(FP8X4),
                rhs_scale=hs[:],
                start=True,
                stop=True,
            )

        def way_back(g):
            y = ring.tile([P, GC], F32, name="y", bufs=2)
            for engine, a, b in Y_PIECES[g]:
                if engine == "S":
                    nc.scalar.copy(y[:, a * C : b * C], ybank[g][:, a * C : b * C])
                else:
                    nc.vector.tensor_copy(y[:, a * C : b * C], ybank[g][:, a * C : b * C])
            nc.vector.tensor_tensor(window[:].indirect(offsets[:, g * GC // 16 : (g + 1) * GC // 16]), y[:], gates[:, group_slots(g)], MULT)

        rows = xT.rearrange("(p j) n -> p j n", j=PACK)
        for g, (first, last) in enumerate(X_GROUPS):
            xg = held.tile([P, (last - first) * C * PACK], BF16, name=f"xg{g}", align_bytes=64)
            grouped.append(xg)
        for u in range(2):
            pair = held.tile([P, 2 * T], BF16, name=f"pair{u}", align_bytes=64)
            pairs.append(pair)
            first = 0
            for width, cut in X_CHUNKS[u]:
                cols = slice(first, first + width)
                first += width
                xraw = ring.tile([P, 2, width], F32, name="xraw", bufs=X_RAW)
                nc.sync.dma_start(xraw[:], rows[:, 2 * u : 2 * u + 2, cols])
                split_copy(
                    pair[:].rearrange("p (t e) -> p t e", e=2)[:, cols, :],
                    xraw[:].rearrange("p e t -> p t e"),
                    cut,
                )
            if u == 0:
                for g in range(len(X_GROUPS)):
                    gather(g, 0)

        load_w1(0)
        load_w2(0)
        load_w1(1)
        load_w1(2)
        load_gates(0)
        load_w1(3)
        gather(0, 1)
        xcodes[0] = quantise(grouped[0], 512, "x0", 1)
        interleave_w1(0)
        load_w1(4)
        layer1(0)
        interleave_w1(1)
        load_w2(4)
        load_w1(5)
        layer1(1)
        interleave_w1(2)
        load_w1(6)
        gather(1, 1)
        layer1(2)
        xcodes[1] = quantise(grouped[1], 1024, "x1", 1)
        interleave_w1(3)
        load_gates(1)
        load_w1(7)
        relu(0)
        layer1(3)
        interleave_w1(4)
        load_w1(8)
        square(0)
        relu(1)
        interleave_w2(0)
        layer1(4)
        interleave_w1(5)
        load_w1(9)
        w2codes[0] = quantise(w2vals[0], W2_RUN * N, "w2", W2_CODES)
        square(1)
        relu(2)
        layer1(5)
        layer2(0)
        interleave_w1(6)
        load_w1(10)
        square(2)
        relu(3)
        layer1(6)
        layer2(1)
        interleave_w1(7)
        load_w1(11)
        load_w2(8)
        load_gates(2)
        square(3)
        relu(4)
        layer1(7)
        layer2(2)
        interleave_w1(8)
        square(4)
        relu(5)
        interleave_w2(4)
        layer1(8)
        layer2(3)
        way_back(0)
        interleave_w1(9)
        w2codes[4] = quantise(w2vals[4], W2_RUN * N, "w2", W2_CODES)
        square(5)
        relu(6)
        layer1(9)
        layer2(4)
        interleave_w1(10)
        square(6)
        relu(7)
        layer1(10)
        layer2(5)
        interleave_w1(11)
        square(7)
        relu(8)
        layer1(11)
        layer2(6)
        square(8)
        relu(9)
        interleave_w2(8)
        layer2(7)
        way_back(1)
        w2codes[8] = quantise(w2vals[8], W2_RUN * N, "w2", W2_CODES)
        square(9)
        relu(10)
        layer2(8)
        square(10)
        relu(11)
        layer2(9)
        square(11)
        layer2(10)
        layer2(11)
        way_back(2)
        nc.sync.dma_start(out, window[:])
